import numpy as np
import ml_dtypes


def mxq(x, axis, fmt="e4m3"):
    dtype, down = {"e4m3": (ml_dtypes.float8_e4m3fn, 7), "e5m2": (ml_dtypes.float8_e5m2, 14)}[fmt]
    v = np.moveaxis(np.asarray(x, np.float32).astype(ml_dtypes.bfloat16).astype(np.float64), axis, -1)
    blocks = v.reshape(v.shape[:-1] + (-1, 32))
    amax = np.abs(blocks).max(-1, keepdims=True)
    byte = np.maximum(np.where(amax > 0, np.frexp(amax)[1] - 1 + 127, 0) - down, 1)
    scale = np.exp2(byte - 127.0)
    codes = (blocks / scale).astype(np.float32).astype(dtype).astype(np.float64)
    return np.moveaxis((codes * scale).reshape(v.shape), -1, axis)


WIDE = False


def mx_kscale(k):
    if not WIDE:
        return np.ones(k)
    levels = np.array([10, -10, 5, -5, 0])
    if k % 512:
        return np.exp2(np.random.permutation(np.resize(levels, k // 32))).repeat(32)
    a = np.empty((k // 512, 16))
    for p in range(k // 512):
        a[p, :8] = np.random.permutation(np.resize(levels, 8))
        for g in range(8):
            far = levels[np.abs(levels - a[p, g]) >= 10]
            a[p, g + 8] = far[np.random.randint(len(far))]
    return np.exp2(a.ravel()).repeat(32)


BF16 = ml_dtypes.bfloat16


def bf(x):
    return np.asarray(x, np.float32).astype(BF16)


def f64(x):
    return np.asarray(x).astype(np.float64)


N, M, D, F = 1024, 1024, 1024, 1024


def tanh_backward(zs, delta):
    h = np.tanh(zs)
    return delta * (1.0 - h * h)


def support_gradient(xs, r):
    return (mxq(xs, 0, "e4m3").T @ mxq(r, 0, "e4m3")) / np.sqrt(N)


def draw0():
    s, t = mx_kscale(N), mx_kscale(D)
    return {
        "xs": bf(np.random.standard_normal((N, D)) * s[:, None]),
        "zs": bf(np.random.standard_normal((N, F))),
        "delta": bf(np.random.standard_normal((N, F)) / s[:, None]),
        "xq": bf(np.random.standard_normal((M, D)) / t),
        "w": bf(np.random.standard_normal((D, F)) / np.sqrt(D)),
        "alpha": bf(np.random.uniform(0.5, 1.5, (D, F)) / np.sqrt(D)),
        "gamma": bf((1.0 + 0.1 * np.random.standard_normal(D)) * t),
    }


def core(xs, zs, delta, xq, w, alpha, gamma):
    r = tanh_backward(f64(zs), f64(delta))
    g = support_gradient(f64(xs), r)
    wp = f64(w) - f64(alpha) * g
    wg = f64(gamma)[:, None] * wp
    return np.tanh(mxq(f64(xq), 1, "e4m3") @ mxq(wg, 0, "e4m3"))


def e4m3fn_bytes(y):
    return np.clip(np.asarray(y, np.float64), -448.0, 448.0).astype(np.float32).astype(ml_dtypes.float8_e4m3fn).view(np.uint8)


def e4m3fn_values(b):
    return np.asarray(b, np.uint8).view(ml_dtypes.float8_e4m3fn).astype(np.float64)


def setup_inputs():
    d = draw0()
    x0 = np.asarray(d['xs']).astype(np.float64)
    s = (np.max(np.abs(x0), axis=(1,), keepdims=True) / 448.0).astype(np.float32)
    out = {}
    for k, v in d.items():
        if k == 'xs':
            out['xs_bytes'] = e4m3fn_bytes(x0 / s.astype(np.float64))
            out['xs_scale'] = s
        else:
            out[k] = v
    return out


def reference(xs_bytes, xs_scale, zs, delta, xq, w, alpha, gamma):
    return core(e4m3fn_values(xs_bytes) * xs_scale.astype(np.float64), zs, delta, xq, w, alpha, gamma)

@@ -1,0 +1,339 @@
+from contextlib import ExitStack
+
+import concourse.mybir as mybir
+from concourse.masks import make_identity
+
+F32 = mybir.dt.float32
+BF16 = mybir.dt.bfloat16
+U32 = mybir.dt.uint32
+U8 = mybir.dt.uint8
+FP8 = mybir.dt.float8_e4m3fn
+FP8X4 = mybir.dt.float8_e4m3fn_x4
+ACT = mybir.ActivationFunctionType
+ALU = mybir.AluOpType
+
+N, M, D, F = 1024, 1024, 1024, 1024
+P = 128
+T = 4
+FH = 512
+RUN = 4
+FLOPS = 2 * N * D * F + 2 * M * D * F
+
+
+def runs(ap):
+    return ap.rearrange("p t (c i) -> p c t i", i=RUN)
+
+
+def tile_metasgdinnerstepqueryforward_kernel(tc, xs_bytes, xs_scale, zs, delta, xq, w, alpha, gamma, out):
+    nc = tc.nc
+    xs_rows = xs_bytes.rearrange("(n p t) d -> n p t d", p=P, t=T)
+    zs_rows = zs.rearrange("(n p t) f -> n p t f", p=P, t=T)
+    delta_rows = delta.rearrange("(n p t) f -> n p t f", p=P, t=T)
+    w_rows = w.rearrange("(g p t) f -> g p t f", p=P, t=T)
+    alpha_rows = alpha.rearrange("(g p t) f -> g p t f", p=P, t=T)
+    xq_rows = xq.rearrange("(q a p) d -> q p a d", a=2, p=P)
+
+    with ExitStack() as ctx:
+        keep = ctx.enter_context(tc.tile_pool(name="keep", bufs=1))
+        ring = ctx.enter_context(tc.tile_pool(name="ring", bufs=2))
+        psum = ctx.enter_context(tc.psum_pool(name="psum", bufs=2))
+        ctx.enter_context(tc.manual_schedule())
+
+        def hold(name, shape, dtype):
+            return keep.tile(shape, dtype, name=name, align_bytes=64)
+
+        scale = hold("scale", [P, 2, 8], F32)
+        gam = hold("gam", [P, 2, 16], BF16)
+        gam32 = hold("gam32", [P, 2, T], F32)
+        ident_f = hold("ident_f", [P, P], F32)
+        ident_b = hold("ident_b", [P, P], BF16)
+        diag = hold("diag", [P, 2 * T, P], BF16)
+        warm = hold("warm", [P, 1], F32)
+        xs_b = [hold("xs_b%d" % n, [P, T, D], U8) for n in range(2)]
+        zs_t = [[hold("zs%d%d" % (n, h), [P, T, FH], BF16) for h in range(2)] for n in range(2)]
+        de_t = [[hold("de%d%d" % (n, h), [P, T, FH], BF16) for h in range(2)] for n in range(2)]
+        al_t = [[hold("al%d%d" % (g, h), [P, T, FH], BF16) for h in range(2)] for g in range(2)]
+        w_t = [[hold("w%d%d" % (g, h), [P, T, FH], BF16) for h in range(2)] for g in range(2)]
+        xq_t = [hold("xq%d" % q, [P, 2, D], BF16) for q in range(4)]
+        xs_c = [[hold("xs_c%d%d" % (n, g), [P, 512], U32) for g in range(2)] for n in range(2)]
+        xs_s = [[hold("xs_s%d%d" % (n, g), [P, 512], U8) for g in range(2)] for n in range(2)]
+        r_c = [[hold("r_c%d%d" % (n, h), [P, FH], U32) for h in range(2)] for n in range(2)]
+        r_s = [[hold("r_s%d%d" % (n, h), [P, FH], U8) for h in range(2)] for n in range(2)]
+        xq_c = [hold("xq_c%d" % q, [P, 2, 2, P], U32) for q in range(4)]
+        xq_s = [hold("xq_s%d" % q, [P, 2, 2, P], U8) for q in range(4)]
+        wg_c = [[hold("wg_c%d%d" % (g, h), [P, FH], U32) for h in range(2)] for g in range(2)]
+        wg_s = [[hold("wg_s%d%d" % (g, h), [P, FH], U8) for h in range(2)] for g in range(2)]
+
+        xs_bf, xs_int, hh, r_int, xq_int, tmp, wg_int, g_ps, wp_ps, o_sb = {}, {}, {}, {}, {}, {}, {}, {}, {}, {}
+
+        def cols(h):
+            return slice(h * FH, (h + 1) * FH)
+
+        def load_half(tiles, rows, n, h):
+            nc.sync.dma_start(out=tiles[n][h][:], in_=rows[n][:, :, cols(h)])
+
+        nc.scalar.dma_start(out=scale[:, :, 0:T], in_=xs_scale.rearrange("(n p t) o -> p n (t o)", p=P, t=T))
+        nc.scalar.dma_start(out=gam[:, :, 0:T], in_=gamma.rearrange("(g p t) -> p g t", p=P, t=T))
+        nc.sync.dma_start(out=xs_b[0][:, 0:2, :], in_=xs_rows[0][:, 0:2, :])
+        nc.sync.dma_start(out=xs_b[0][:, 2:4, :], in_=xs_rows[0][:, 2:4, :])
+        load_half(zs_t, zs_rows, 0, 0)
+        nc.sync.dma_start(out=xs_b[1][:], in_=xs_rows[1])
+        load_half(zs_t, zs_rows, 1, 0)
+        for n in range(2):
+            load_half(de_t, delta_rows, n, 0)
+        load_half(al_t, alpha_rows, 0, 0)
+        load_half(w_t, w_rows, 0, 0)
+        for n in range(2):
+            load_half(zs_t, zs_rows, n, 1)
+        load_half(al_t, alpha_rows, 1, 0)
+        load_half(w_t, w_rows, 1, 0)
+        for q in range(4):
+            nc.sync.dma_start(out=xq_t[q][:], in_=xq_rows[q])
+        for n in range(2):
+            load_half(de_t, delta_rows, n, 1)
+        for g in range(2):
+            load_half(al_t, alpha_rows, g, 1)
+            load_half(w_t, w_rows, g, 1)
+
+        def setup():
+            nc.gpsimd.memset(warm[:], 0.0)
+            make_identity(nc, ident_f[:])
+            make_identity(nc, ident_b[:])
+            nc.scalar.activation(out=warm[:], in_=warm[:], func=ACT.Tanh)
+
+        def setup_gamma():
+            nc.vector.tensor_scalar(out=gam32[:], in0=gam[:, :, 0:T], scalar1=1.0 / 32.0, scalar2=None, op0=ALU.mult)
+            nc.vector.tensor_tensor(
+                out=diag[:].rearrange("p (g t) c -> p g t c", g=2),
+                in0=ident_b[:].unsqueeze(1).unsqueeze(1).to_broadcast([P, 2, T, P]),
+                in1=gam[:, :, 0:T].unsqueeze(3).to_broadcast([P, 2, T, P]),
+                op=ALU.mult,
+            )
+
+        def dequant(n, g, engine):
+            if (n, g) not in xs_bf:
+                xs_bf[n, g] = ring.tile([P, T, 512], BF16, name="xs_bf", bufs=3, align_bytes=64)
+            for t in range(T):
+                src = xs_b[n][:, t, g * 512 : (g + 1) * 512].bitcast(FP8)
+                dst = xs_bf[n, g][:, t, :]
+                col = scale[:, n, t : t + 1]
+                if engine == "v":
+                    nc.vector.tensor_scalar(out=dst, in0=src, scalar1=col, scalar2=None, op0=ALU.mult)
+                else:
+                    nc.scalar.activation(out=dst, in_=src, func=ACT.Copy, scale=col)
+
+        def xs_interleave(n, g):
+            xs_int[n, g] = ring.tile([P, 512 * T], BF16, name="xs_int", bufs=2, align_bytes=64)
+            nc.vector.tensor_copy(
+                out=xs_int[n, g][:].rearrange("p (t m j) -> p t m j", t=T, j=T),
+                in_=xs_bf[n, g][:].rearrange("p j (m t) -> p t m j", t=T),
+            )
+
+        def xs_quant(n, g):
+            nc.vector.quantize_mx(out=xs_c[n][g][:].bitcast(FP8X4), scales=xs_s[n][g][:], in_=xs_int[n, g][:])
+
+        def tanh_z(n, h):
+            hh[n, h] = ring.tile([P, T, FH], F32, name="hh", bufs=3, align_bytes=64)
+            nc.scalar.activation(out=hh[n, h][:], in_=zs_t[n][h][:], func=ACT.Tanh)
+
+        def square_z(n, h):
+            nc.scalar.activation(out=hh[n, h][:], in_=hh[n, h][:], func=ACT.Square)
+
+        def r_mul(n, h):
+            r_int[n, h] = ring.tile([P, FH, T], BF16, name="r_int", bufs=2, align_bytes=64)
+            nc.vector.scalar_tensor_tensor(
+                out=r_int[n, h][:], in0=hh[n, h][:].rearrange("p t f -> p f t"), scalar=1.0,
+                in1=de_t[n][h][:].rearrange("p t f -> p f t"), op0=ALU.subtract, op1=ALU.mult,
+            )
+
+        def r_quant(n, h):
+            nc.vector.quantize_mx(
+                out=r_c[n][h][:].bitcast(FP8X4), scales=r_s[n][h][:], in_=r_int[n, h][:].rearrange("p f t -> p (f t)")
+            )
+
+        def g_matmul(g, h, t):
+            g_ps[g, h, t] = psum.tile([P, FH], F32, name="g_ps", bufs=3)
+            c = slice(t * P, (t + 1) * P)
+            for n in range(2):
+                nc.tensor.matmul_mx(
+                    out=g_ps[g, h, t][:], lhsT=xs_c[n][g][:, c].bitcast(FP8X4), lhsT_scale=xs_s[n][g][:, c],
+                    rhs=r_c[n][h][:].bitcast(FP8X4), rhs_scale=r_s[n][h][:], start=(n == 0), stop=(n == 1),
+                )
+
+        def w_scaled(g, h, j):
+            wp_ps[g, h, j] = psum.tile([P, T, P], F32, name="wp_ps", bufs=2)
+            for t in range(T):
+                nc.tensor.matmul(
+                    wp_ps[g, h, j][:, t, :], lhsT=diag[:, g * T + t, :], rhs=w_t[g][h][:, t, j * P : (j + 1) * P],
+                    start=True, stop=True,
+                )
+
+        def upd_mul(g, h, t):
+            if t == 0:
+                tmp[g, h] = ring.tile([P, T, FH], F32, name="tmp", bufs=2, align_bytes=64)
+            nc.vector.scalar_tensor_tensor(
+                out=tmp[g, h][:, t, :], in0=g_ps[g, h, t][:], scalar=gam32[:, g, t : t + 1], in1=al_t[g][h][:, t, :],
+                op0=ALU.mult, op1=ALU.mult,
+            )
+
+        def upd_add(g, h, j):
+            if j == 0:
+                wg_int[g, h] = ring.tile([P, FH, T], BF16, name="wg_int", bufs=2, align_bytes=64)
+            f = slice(j * P, (j + 1) * P)
+            nc.vector.tensor_tensor(
+                out=wg_int[g, h][:, f, :].rearrange("p (c i) t -> p c t i", i=RUN),
+                in0=runs(wp_ps[g, h, j][:]), in1=runs(tmp[g, h][:, :, f]), op=ALU.add,
+            )
+
+        def wg_quant(g, h, j0, j1):
+            f = slice(j0 * P, j1 * P)
+            nc.vector.quantize_mx(
+                out=wg_c[g][h][:, f].bitcast(FP8X4), scales=wg_s[g][h][:, f],
+                in_=wg_int[g, h][:, f, :].rearrange("p f t -> p (f t)"),
+            )
+
+        def xq_turn(m):
+            q, a = divmod(m, 2)
+            bank = psum.tile([P, 2, 2, P], F32, name="o_ps", bufs=3)
+            words = xq_t[q][:, a, :].bitcast(F32)
+            for g in range(2):
+                for u in range(2):
+                    nc.tensor.transpose(bank[:, g, u, :], words[:, 256 * g + u : 256 * (g + 1) : 2], ident_f[:])
+            if a == 0:
+                xq_int[q] = ring.tile([P, 2, 2, P, T], BF16, name="xq_int", bufs=2, align_bytes=64)
+            nc.scalar.copy(
+                out=xq_int[q][:, a].rearrange("p g r t -> p (g r t)").bitcast(F32).rearrange("p (g r u) -> p g r u", g=2, u=2),
+                in_=bank[:].rearrange("p g u r -> p g r u"),
+            )
+
+        def xq_quant(q):
+            nc.vector.quantize_mx(
+                out=xq_c[q][:].rearrange("p a g r -> p (a g r)").bitcast(FP8X4),
+                scales=xq_s[q][:].rearrange("p a g r -> p (a g r)"),
+                in_=xq_int[q][:].rearrange("p a g r t -> p (a g r t)"),
+            )
+
+        def out_pass(ps, m, g, h, f):
+            q, a = divmod(m, 2)
+            nc.tensor.matmul_mx(
+                out=ps, lhsT=xq_c[q][:, a, g, :].bitcast(FP8X4), lhsT_scale=xq_s[q][:, a, g, :],
+                rhs=wg_c[g][h][:, f].bitcast(FP8X4), rhs_scale=wg_s[g][h][:, f], start=(g == 0), stop=(g == 1),
+            )
+
+        def out_wide(m, h):
+            bank = psum.tile([P, FH], F32, name="o_ps", bufs=3)
+            for g in range(2):
+                out_pass(bank[:], m, g, h, slice(0, FH))
+            res = ring.tile([P, FH], F32, name="res", bufs=4, align_bytes=64)
+            nc.scalar.activation(out=res[:], in_=bank[:], func=ACT.Tanh)
+            nc.sync.dma_start(out=out[m * P : (m + 1) * P, cols(h)], in_=res[:])
+
+        def out_pair(q, h, s):
+            bank = psum.tile([P, 2, 256], F32, name="o_ps", bufs=3)
+            for a in range(2):
+                for g in range(2):
+                    out_pass(bank[:, a, :], 2 * q + a, g, h, slice(256 * s, 256 * (s + 1)))
+            res = ring.tile([P, 2, 256], F32, name="res", bufs=4, align_bytes=64)
+            nc.scalar.activation(out=res[:], in_=bank[:], func=ACT.Tanh)
+            nc.sync.dma_start(
+                out=out.rearrange("(q a p) f -> q p a f", a=2, p=P)[q][:, :, h * FH + 256 * s : h * FH + 256 * (s + 1)], in_=res[:]
+            )
+
+        setup()
+        dequant(0, 0, "v")
+        tanh_z(0, 0)
+        square_z(0, 0)
+        xs_interleave(0, 0)
+        dequant(1, 0, "v")
+        xs_quant(0, 0)
+        setup_gamma()
+        xs_interleave(1, 0)
+        tanh_z(1, 0)
+        square_z(1, 0)
+        r_mul(0, 0)
+        xs_quant(1, 0)
+        dequant(0, 1, "s")
+        dequant(1, 1, "s")
+        r_mul(1, 0)
+        r_quant(0, 0)
+        xs_interleave(0, 1)
+        r_quant(1, 0)
+        tanh_z(0, 1)
+        square_z(0, 1)
+        tanh_z(1, 1)
+        square_z(1, 1)
+        for t in range(3):
+            g_matmul(0, 0, t)
+        w_scaled(0, 0, 0)
+        w_scaled(0, 0, 1)
+        xs_interleave(1, 1)
+        xs_quant(0, 1)
+        upd_mul(0, 0, 0)
+        upd_mul(0, 0, 1)
+        upd_mul(0, 0, 2)
+        g_matmul(0, 0, 3)
+        upd_mul(0, 0, 3)
+        xs_quant(1, 1)
+        for t in range(2):
+            g_matmul(1, 0, t)
+        for t in range(4):
+            upd_add(0, 0, t)
+            if t < 2:
+                w_scaled(0, 0, t + 2)
+            else:
+                w_scaled(1, 0, t - 2)
+            upd_mul(1, 0, t)
+            if t < 2:
+                g_matmul(1, 0, t + 2)
+        for m in range(4):
+            xq_turn(m)
+        wg_quant(0, 0, 0, 4)
+        for j in range(4):
+            upd_add(1, 0, j)
+            if j < 2:
+                w_scaled(1, 0, j + 2)
+        xq_quant(0)
+        xq_quant(1)
+        wg_quant(1, 0, 0, 4)
+        for m in range(4, 8):
+            xq_turn(m)
+        r_mul(0, 1)
+        xq_quant(2)
+        r_mul(1, 1)
+        r_quant(0, 1)
+        xq_quant(3)
+        r_quant(1, 1)
+        for m in range(4):
+            out_wide(m, 0)
+        for t in range(3):
+            g_matmul(0, 1, t)
+        w_scaled(0, 1, 0)
+        w_scaled(0, 1, 1)
+        for t in range(4):
+            if t == 1:
+                g_matmul(0, 1, 3)
+            upd_mul(0, 1, t)
+        for m in range(4, 6):
+            out_wide(m, 0)
+        for t in range(2):
+            g_matmul(1, 1, t)
+        for t in range(4):
+            upd_add(0, 1, t)
+            if t < 2:
+                w_scaled(0, 1, t + 2)
+            else:
+                w_scaled(1, 1, t - 2)
+            upd_mul(1, 1, t)
+            if t < 2:
+                g_matmul(1, 1, t + 2)
+        for m in range(6, 8):
+            out_wide(m, 0)
+        for s in range(2):
+            for j in (2 * s, 2 * s + 1):
+                upd_add(1, 1, j)
+                if s == 0:
+                    w_scaled(1, 1, j + 2)
+            wg_quant(0, 1, 2 * s, 2 * s + 2)
+            wg_quant(1, 1, 2 * s, 2 * s + 2)
+            for q in range(4):
+                out_pair(q, 1, s)

@@ -37,7 +37,7 @@ def tile_metasgdinnerstepqueryforward_kernel(tc, xs_bytes, xs_scale, zs, delta, 
         keep = ctx.enter_context(tc.tile_pool(name="keep", bufs=1))
         ring = ctx.enter_context(tc.tile_pool(name="ring", bufs=2))
         psum = ctx.enter_context(tc.psum_pool(name="psum", bufs=2))
-        ctx.enter_context(tc.manual_schedule())
+        ctx.enter_context(tc.manual_schedule(engines={mybir.EngineType.DVE, mybir.EngineType.Activation, mybir.EngineType.SP, mybir.EngineType.Pool}))
 
         def hold(name, shape, dtype):
             return keep.tile(shape, dtype, name=name, align_bytes=64)
@@ -55,14 +55,15 @@ def tile_metasgdinnerstepqueryforward_kernel(tc, xs_bytes, xs_scale, zs, delta, 
         al_t = [[hold("al%d%d" % (g, h), [P, T, FH], BF16) for h in range(2)] for g in range(2)]
         w_t = [[hold("w%d%d" % (g, h), [P, T, FH], BF16) for h in range(2)] for g in range(2)]
         xq_t = [hold("xq%d" % q, [P, 2, D], BF16) for q in range(4)]
-        xs_c = [[hold("xs_c%d%d" % (n, g), [P, 512], U32) for g in range(2)] for n in range(2)]
-        xs_s = [[hold("xs_s%d%d" % (n, g), [P, 512], U8) for g in range(2)] for n in range(2)]
+        xs_c = [hold("xs_c%d" % n, [P, D], U32) for n in range(2)]
+        xs_s = [hold("xs_s%d" % n, [P, D], U8) for n in range(2)]
         r_c = [[hold("r_c%d%d" % (n, h), [P, FH], U32) for h in range(2)] for n in range(2)]
         r_s = [[hold("r_s%d%d" % (n, h), [P, FH], U8) for h in range(2)] for n in range(2)]
-        xq_c = [hold("xq_c%d" % q, [P, 2, 2, P], U32) for q in range(4)]
-        xq_s = [hold("xq_s%d" % q, [P, 2, 2, P], U8) for q in range(4)]
+        xq_c = [hold("xq_c%d" % q, [P, 4, 2, P], U32) for q in range(2)]
+        xq_s = [hold("xq_s%d" % q, [P, 4, 2, P], U8) for q in range(2)]
         wg_c = [[hold("wg_c%d%d" % (g, h), [P, FH], U32) for h in range(2)] for g in range(2)]
         wg_s = [[hold("wg_s%d%d" % (g, h), [P, FH], U8) for h in range(2)] for g in range(2)]
+        CHUNK = [(0, 0, 512), (1, 0, 512)]
 
         xs_bf, xs_int, hh, r_int, xq_int, tmp, wg_int, g_ps, wp_ps, o_sb = {}, {}, {}, {}, {}, {}, {}, {}, {}, {}
 
@@ -74,9 +75,9 @@ def tile_metasgdinnerstepqueryforward_kernel(tc, xs_bytes, xs_scale, zs, delta, 
 
         nc.scalar.dma_start(out=scale[:, :, 0:T], in_=xs_scale.rearrange("(n p t) o -> p n (t o)", p=P, t=T))
         nc.scalar.dma_start(out=gam[:, :, 0:T], in_=gamma.rearrange("(g p t) -> p g t", p=P, t=T))
-        nc.sync.dma_start(out=xs_b[0][:, 0:2, :], in_=xs_rows[0][:, 0:2, :])
-        nc.sync.dma_start(out=xs_b[0][:, 2:4, :], in_=xs_rows[0][:, 2:4, :])
-        load_half(zs_t, zs_rows, 0, 0)
+        for t in (slice(0, 2), slice(2, 4)):
+            nc.sync.dma_start(out=xs_b[0][:, t, :], in_=xs_rows[0][:, t, :])
+            nc.sync.dma_start(out=zs_t[0][0][:, t, :], in_=zs_rows[0][:, t, cols(0)])
         nc.sync.dma_start(out=xs_b[1][:], in_=xs_rows[1])
         load_half(zs_t, zs_rows, 1, 0)
         for n in range(2):
@@ -101,8 +102,10 @@ def tile_metasgdinnerstepqueryforward_kernel(tc, xs_bytes, xs_scale, zs, delta, 
             make_identity(nc, ident_b[:])
             nc.scalar.activation(out=warm[:], in_=warm[:], func=ACT.Tanh)
 
-        def setup_gamma():
+        def gamma_columns():
             nc.vector.tensor_scalar(out=gam32[:], in0=gam[:, :, 0:T], scalar1=1.0 / 32.0, scalar2=None, op0=ALU.mult)
+
+        def gamma_diagonals():
             nc.vector.tensor_tensor(
                 out=diag[:].rearrange("p (g t) c -> p g t c", g=2),
                 in0=ident_b[:].unsqueeze(1).unsqueeze(1).to_broadcast([P, 2, T, P]),
@@ -110,31 +113,43 @@ def tile_metasgdinnerstepqueryforward_kernel(tc, xs_bytes, xs_scale, zs, delta, 
                 op=ALU.mult,
             )
 
-        def dequant(n, g, engine):
-            if (n, g) not in xs_bf:
-                xs_bf[n, g] = ring.tile([P, T, 512], BF16, name="xs_bf", bufs=3, align_bytes=64)
-            for t in range(T):
-                src = xs_b[n][:, t, g * 512 : (g + 1) * 512].bitcast(FP8)
-                dst = xs_bf[n, g][:, t, :]
-                col = scale[:, n, t : t + 1]
-                if engine == "v":
-                    nc.vector.tensor_scalar(out=dst, in0=src, scalar1=col, scalar2=None, op0=ALU.mult)
-                else:
-                    nc.scalar.activation(out=dst, in_=src, func=ACT.Copy, scale=col)
+        def dequant(n, t, engine, d=slice(0, D)):
+            if n not in xs_bf:
+                xs_bf[n] = ring.tile([P, T, D], BF16, name="xs_bf", tag="big", bufs=6, align_bytes=64)
+            src = xs_b[n][:, t, d].bitcast(FP8)
+            dst = xs_bf[n][:, t, d]
+            col = scale[:, n, t : t + 1]
+            if engine == "v":
+                nc.vector.tensor_scalar(out=dst, in0=src, scalar1=col, scalar2=None, op0=ALU.mult)
+            else:
+                nc.scalar.activation(out=dst, in_=src, func=ACT.Copy, scale=col)
 
-        def xs_interleave(n, g):
-            xs_int[n, g] = ring.tile([P, 512 * T], BF16, name="xs_int", bufs=2, align_bytes=64)
-            nc.vector.tensor_copy(
-                out=xs_int[n, g][:].rearrange("p (t m j) -> p t m j", t=T, j=T),
-                in_=xs_bf[n, g][:].rearrange("p j (m t) -> p t m j", t=T),
-            )
+        def xs_interleave(n, g, engine="v"):
+            if n == 0:
+                xs_int[n] = ring.tile([P, D * T], BF16, name="xs_int0", tag="big", bufs=6, align_bytes=64)
+                o = xs_int[n][:].rearrange("p (t m j) -> p m j t", t=T, j=T)
+                i = xs_bf[n][:].rearrange("p j (m t) -> p m j t", t=T)
+            else:
+                if n not in xs_int:
+                    xs_int[n] = ring.tile([P, 2, 512 * T], BF16, name="xs_int1", tag="big", bufs=6, align_bytes=64)
+                o = xs_int[n][:, g, :].rearrange("p (t m j) -> p m j t", t=T, j=T)
+                i = xs_bf[n][:, :, g * 512 : (g + 1) * 512].rearrange("p j (m t) -> p m j t", t=T)
+            if engine == "v":
+                nc.vector.tensor_copy(out=o, in_=i)
+            else:
+                nc.scalar.copy(out=o, in_=i)
 
         def xs_quant(n, g):
-            nc.vector.quantize_mx(out=xs_c[n][g][:].bitcast(FP8X4), scales=xs_s[n][g][:], in_=xs_int[n, g][:])
+            c = slice(0, D) if n == 0 else slice(g * 512, (g + 1) * 512)
+            src = xs_int[n][:] if n == 0 else xs_int[n][:, g, :]
+            nc.vector.quantize_mx(out=xs_c[n][:, c].bitcast(FP8X4), scales=xs_s[n][:, c], in_=src)
 
-        def tanh_z(n, h):
+        def tanh_z(n, h, parts=1):
             hh[n, h] = ring.tile([P, T, FH], F32, name="hh", bufs=3, align_bytes=64)
-            nc.scalar.activation(out=hh[n, h][:], in_=zs_t[n][h][:], func=ACT.Tanh)
+            k = T // parts
+            for a in range(parts):
+                t = slice(a * k, (a + 1) * k)
+                nc.scalar.activation(out=hh[n, h][:, t, :], in_=zs_t[n][h][:, t, :], func=ACT.Tanh)
 
         def square_z(n, h):
             nc.scalar.activation(out=hh[n, h][:], in_=hh[n, h][:], func=ACT.Square)
@@ -151,56 +166,73 @@ def tile_metasgdinnerstepqueryforward_kernel(tc, xs_bytes, xs_scale, zs, delta, 
                 out=r_c[n][h][:].bitcast(FP8X4), scales=r_s[n][h][:], in_=r_int[n, h][:].rearrange("p f t -> p (f t)")
             )
 
-        def g_matmul(g, h, t):
-            g_ps[g, h, t] = psum.tile([P, FH], F32, name="g_ps", bufs=3)
-            c = slice(t * P, (t + 1) * P)
+        def g_matmul(g, c, t):
+            h, f0, width = CHUNK[c]
+            f = slice(f0, f0 + width)
+            g_ps[g, c, t] = psum.tile([P, width], F32, name="g_ps", bufs=3)
             for n in range(2):
+                d0 = (2 * t + g) * P if n == 0 else (4 * g + t) * P
+                d = slice(d0, d0 + P)
                 nc.tensor.matmul_mx(
-                    out=g_ps[g, h, t][:], lhsT=xs_c[n][g][:, c].bitcast(FP8X4), lhsT_scale=xs_s[n][g][:, c],
-                    rhs=r_c[n][h][:].bitcast(FP8X4), rhs_scale=r_s[n][h][:], start=(n == 0), stop=(n == 1),
+                    out=g_ps[g, c, t][:], lhsT=xs_c[n][:, d].bitcast(FP8X4), lhsT_scale=xs_s[n][:, d],
+                    rhs=r_c[n][h][:, f].bitcast(FP8X4), rhs_scale=r_s[n][h][:, f], start=(n == 0), stop=(n == 1),
                 )
 
-        def w_scaled(g, h, j):
-            wp_ps[g, h, j] = psum.tile([P, T, P], F32, name="wp_ps", bufs=2)
+        def w_scaled(g, c, j, full=False):
+            h, f0, width = CHUNK[c]
+            wp_ps[g, c, j] = psum.tile([P, T, P], F32, name="wp_ps", bufs=2)
             for t in range(T):
                 nc.tensor.matmul(
-                    wp_ps[g, h, j][:, t, :], lhsT=diag[:, g * T + t, :], rhs=w_t[g][h][:, t, j * P : (j + 1) * P],
-                    start=True, stop=True,
+                    wp_ps[g, c, j][:, t, :], lhsT=diag[:, g * T + t, :], rhs=w_t[g][h][:, t, f0 + j * P : f0 + (j + 1) * P],
+                    start=True, stop=not full,
                 )
+                if full:
+                    nc.tensor.matmul(
+                        wp_ps[g, c, j][:, t, :], lhsT=ident_f[:], rhs=tmp[g, c][:, t, j * P : (j + 1) * P],
+                        start=False, stop=True,
+                    )
 
-        def upd_mul(g, h, t):
+        def upd_mul(g, c, t):
+            h, f0, width = CHUNK[c]
             if t == 0:
-                tmp[g, h] = ring.tile([P, T, FH], F32, name="tmp", bufs=2, align_bytes=64)
+                tmp[g, c] = ring.tile([P, T, width], F32, name="tmp", tag="big", bufs=6, align_bytes=64)
             nc.vector.scalar_tensor_tensor(
-                out=tmp[g, h][:, t, :], in0=g_ps[g, h, t][:], scalar=gam32[:, g, t : t + 1], in1=al_t[g][h][:, t, :],
-                op0=ALU.mult, op1=ALU.mult,
+                out=tmp[g, c][:, t, :], in0=g_ps[g, c, t][:], scalar=gam32[:, g, t : t + 1],
+                in1=al_t[g][h][:, t, f0 : f0 + width], op0=ALU.mult, op1=ALU.mult,
             )
 
-        def upd_add(g, h, j):
-            if j == 0:
-                wg_int[g, h] = ring.tile([P, FH, T], BF16, name="wg_int", bufs=2, align_bytes=64)
-            f = slice(j * P, (j + 1) * P)
+        def wg_piece(g, c, j):
+            h, f0, width = CHUNK[c]
+            if (g, c) not in wg_int:
+                wg_int[g, c] = ring.tile([P, width, T], BF16, name="wg_int", bufs=2, align_bytes=64)
+            return wg_int[g, c][:, j * P : (j + 1) * P, :]
+
+        def upd_add(g, c, j):
             nc.vector.tensor_tensor(
-                out=wg_int[g, h][:, f, :].rearrange("p (c i) t -> p c t i", i=RUN),
-                in0=runs(wp_ps[g, h, j][:]), in1=runs(tmp[g, h][:, :, f]), op=ALU.add,
+                out=wg_piece(g, c, j).rearrange("p (c i) t -> p c t i", i=RUN),
+                in0=runs(wp_ps[g, c, j][:]), in1=runs(tmp[g, c][:, :, j * P : (j + 1) * P]), op=ALU.add,
             )
 
-        def wg_quant(g, h, j0, j1):
-            f = slice(j0 * P, j1 * P)
+        def upd_out(g, c, j):
+            nc.scalar.copy(out=wg_piece(g, c, j), in_=wp_ps[g, c, j][:].rearrange("p t f -> p f t"))
+
+        def wg_quant(g, c, j0, j1):
+            h, f0, width = CHUNK[c]
+            f = slice(f0 + j0 * P, f0 + j1 * P)
             nc.vector.quantize_mx(
                 out=wg_c[g][h][:, f].bitcast(FP8X4), scales=wg_s[g][h][:, f],
-                in_=wg_int[g, h][:, f, :].rearrange("p f t -> p (f t)"),
+                in_=wg_int[g, c][:, j0 * P : j1 * P, :].rearrange("p f t -> p (f t)"),
             )
 
         def xq_turn(m):
-            q, a = divmod(m, 2)
+            q, a = divmod(m, 4)
             bank = psum.tile([P, 2, 2, P], F32, name="o_ps", bufs=3)
-            words = xq_t[q][:, a, :].bitcast(F32)
+            words = xq_t[m // 2][:, m % 2, :].bitcast(F32)
             for g in range(2):
                 for u in range(2):
                     nc.tensor.transpose(bank[:, g, u, :], words[:, 256 * g + u : 256 * (g + 1) : 2], ident_f[:])
             if a == 0:
-                xq_int[q] = ring.tile([P, 2, 2, P, T], BF16, name="xq_int", bufs=2, align_bytes=64)
+                xq_int[q] = ring.tile([P, 4, 2, P, T], BF16, name="xq_int", tag="big", bufs=6, align_bytes=64)
             nc.scalar.copy(
                 out=xq_int[q][:, a].rearrange("p g r t -> p (g r t)").bitcast(F32).rearrange("p (g r u) -> p g r u", g=2, u=2),
                 in_=bank[:].rearrange("p g u r -> p g r u"),
@@ -213,61 +245,51 @@ def tile_metasgdinnerstepqueryforward_kernel(tc, xs_bytes, xs_scale, zs, delta, 
                 in_=xq_int[q][:].rearrange("p a g r t -> p (a g r t)"),
             )
 
-        def out_pass(ps, m, g, h, f):
-            q, a = divmod(m, 2)
-            nc.tensor.matmul_mx(
-                out=ps, lhsT=xq_c[q][:, a, g, :].bitcast(FP8X4), lhsT_scale=xq_s[q][:, a, g, :],
-                rhs=wg_c[g][h][:, f].bitcast(FP8X4), rhs_scale=wg_s[g][h][:, f], start=(g == 0), stop=(g == 1),
-            )
-
-        def out_wide(m, h):
-            bank = psum.tile([P, FH], F32, name="o_ps", bufs=3)
-            for g in range(2):
-                out_pass(bank[:], m, g, h, slice(0, FH))
-            res = ring.tile([P, FH], F32, name="res", bufs=4, align_bytes=64)
-            nc.scalar.activation(out=res[:], in_=bank[:], func=ACT.Tanh)
-            nc.sync.dma_start(out=out[m * P : (m + 1) * P, cols(h)], in_=res[:])
-
-        def out_pair(q, h, s):
-            bank = psum.tile([P, 2, 256], F32, name="o_ps", bufs=3)
-            for a in range(2):
+        def out_block(m0, h, f0, width):
+            k = 512 // width
+            bank = psum.tile([P, k, width], F32, name="o_ps", bufs=3)
+            f = slice(f0, f0 + width)
+            for b in range(k):
+                q, a = divmod(m0 + b, 4)
                 for g in range(2):
-                    out_pass(bank[:, a, :], 2 * q + a, g, h, slice(256 * s, 256 * (s + 1)))
-            res = ring.tile([P, 2, 256], F32, name="res", bufs=4, align_bytes=64)
+                    nc.tensor.matmul_mx(
+                        out=bank[:, b, :], lhsT=xq_c[q][:, a, g, :].bitcast(FP8X4), lhsT_scale=xq_s[q][:, a, g, :],
+                        rhs=wg_c[g][h][:, f].bitcast(FP8X4), rhs_scale=wg_s[g][h][:, f], start=(g == 0), stop=(g == 1),
+                    )
+            res = ring.tile([P, k, width], F32, name="res", bufs=8, align_bytes=64)
             nc.scalar.activation(out=res[:], in_=bank[:], func=ACT.Tanh)
-            nc.sync.dma_start(
-                out=out.rearrange("(q a p) f -> q p a f", a=2, p=P)[q][:, :, h * FH + 256 * s : h * FH + 256 * (s + 1)], in_=res[:]
-            )
+            rows = out[m0 * P : (m0 + k) * P, h * FH + f0 : h * FH + f0 + width]
+            nc.sync.dma_start(out=rows.rearrange("(b p) f -> p b f", p=P), in_=res[:])
 
         setup()
-        dequant(0, 0, "v")
-        tanh_z(0, 0)
+        tanh_z(0, 0, 2)
         square_z(0, 0)
+        for t in range(4):
+            dequant(0, t, "v")
         xs_interleave(0, 0)
         dequant(1, 0, "v")
+        dequant(1, 1, "v")
         xs_quant(0, 0)
-        setup_gamma()
-        xs_interleave(1, 0)
+        gamma_columns()
         tanh_z(1, 0)
         square_z(1, 0)
         r_mul(0, 0)
-        xs_quant(1, 0)
-        dequant(0, 1, "s")
-        dequant(1, 1, "s")
+        for g in range(2):
+            for t in range(2, 4):
+                dequant(1, t, "s", slice(512 * g, 512 * (g + 1)))
         r_mul(1, 0)
         r_quant(0, 0)
-        xs_interleave(0, 1)
+        xs_interleave(1, 0)
         r_quant(1, 0)
+        xs_quant(1, 0)
+        gamma_diagonals()
+        xs_interleave(1, 1, "s")
         tanh_z(0, 1)
         square_z(0, 1)
-        tanh_z(1, 1)
-        square_z(1, 1)
         for t in range(3):
             g_matmul(0, 0, t)
         w_scaled(0, 0, 0)
         w_scaled(0, 0, 1)
-        xs_interleave(1, 1)
-        xs_quant(0, 1)
         upd_mul(0, 0, 0)
         upd_mul(0, 0, 1)
         upd_mul(0, 0, 2)
@@ -280,11 +302,10 @@ def tile_metasgdinnerstepqueryforward_kernel(tc, xs_bytes, xs_scale, zs, delta, 
             upd_add(0, 0, t)
             if t < 2:
                 w_scaled(0, 0, t + 2)
+                g_matmul(1, 0, t + 2)
             else:
                 w_scaled(1, 0, t - 2)
             upd_mul(1, 0, t)
-            if t < 2:
-                g_matmul(1, 0, t + 2)
         for m in range(4):
             xq_turn(m)
         wg_quant(0, 0, 0, 4)
@@ -292,48 +313,57 @@ def tile_metasgdinnerstepqueryforward_kernel(tc, xs_bytes, xs_scale, zs, delta, 
             upd_add(1, 0, j)
             if j < 2:
                 w_scaled(1, 0, j + 2)
-        xq_quant(0)
-        xq_quant(1)
-        wg_quant(1, 0, 0, 4)
+        tanh_z(1, 1)
         for m in range(4, 8):
             xq_turn(m)
+        square_z(1, 1)
+        xq_quant(0)
+        wg_quant(1, 0, 0, 4)
         r_mul(0, 1)
-        xq_quant(2)
-        r_mul(1, 1)
+        xq_quant(1)
         r_quant(0, 1)
-        xq_quant(3)
+        r_mul(1, 1)
+        for m in range(2):
+            out_block(m, 0, 0, 512)
         r_quant(1, 1)
-        for m in range(4):
-            out_wide(m, 0)
+        for m in range(2, 6):
+            out_block(m, 0, 0, 512)
         for t in range(3):
             g_matmul(0, 1, t)
         w_scaled(0, 1, 0)
         w_scaled(0, 1, 1)
         for t in range(4):
-            if t == 1:
-                g_matmul(0, 1, 3)
             upd_mul(0, 1, t)
-        for m in range(4, 6):
-            out_wide(m, 0)
-        for t in range(2):
-            g_matmul(1, 1, t)
-        for t in range(4):
-            upd_add(0, 1, t)
-            if t < 2:
-                w_scaled(0, 1, t + 2)
-            else:
-                w_scaled(1, 1, t - 2)
-            upd_mul(1, 1, t)
-            if t < 2:
-                g_matmul(1, 1, t + 2)
+            if t == 0:
+                g_matmul(0, 1, 3)
+            elif t < 3:
+                g_matmul(1, 1, t - 1)
         for m in range(6, 8):
-            out_wide(m, 0)
-        for s in range(2):
-            for j in (2 * s, 2 * s + 1):
-                upd_add(1, 1, j)
-                if s == 0:
-                    w_scaled(1, 1, j + 2)
-            wg_quant(0, 1, 2 * s, 2 * s + 2)
-            wg_quant(1, 1, 2 * s, 2 * s + 2)
-            for q in range(4):
-                out_pair(q, 1, s)
+            out_block(m, 0, 0, 512)
+        for t in range(4):
+            if t < 2:
+                upd_add(0, 1, t)
+                w_scaled(1, 1, t)
+                g_matmul(1, 1, t + 2)
+            upd_mul(1, 1, t)
+        wg_quant(0, 1, 0, 2)
+        upd_add(1, 1, 0)
+        w_scaled(0, 1, 2)
+        w_scaled(0, 1, 3)
+        upd_add(1, 1, 1)
+        upd_add(0, 1, 2)
+        w_scaled(1, 1, 2)
+        wg_quant(1, 1, 0, 2)
+        upd_add(0, 1, 3)
+        w_scaled(1, 1, 3)
+        for m in range(0, 8, 2):
+            out_block(m, 1, 0, 256)
+        wg_quant(0, 1, 2, 4)
+        upd_add(1, 1, 2)
+        wg_quant(1, 1, 2, 3)
+        upd_add(1, 1, 3)
+        for m in range(0, 8, 4):
+            out_block(m, 1, 256, 128)
+        wg_quant(1, 1, 3, 4)
+        for m in range(0, 8, 4):
+            out_block(m, 1, 384, 128)

@@ -37,13 +37,14 @@ def tile_metasgdinnerstepqueryforward_kernel(tc, xs_bytes, xs_scale, zs, delta, 
         keep = ctx.enter_context(tc.tile_pool(name="keep", bufs=1))
         ring = ctx.enter_context(tc.tile_pool(name="ring", bufs=2))
         psum = ctx.enter_context(tc.psum_pool(name="psum", bufs=2))
-        ctx.enter_context(tc.manual_schedule(engines={mybir.EngineType.DVE, mybir.EngineType.Activation, mybir.EngineType.SP, mybir.EngineType.Pool}))
+        ctx.enter_context(tc.manual_schedule())
 
         def hold(name, shape, dtype):
             return keep.tile(shape, dtype, name=name, align_bytes=64)
 
         scale = hold("scale", [P, 2, 8], F32)
         gam = hold("gam", [P, 2, 16], BF16)
+        gam1 = hold("gam1", [P, 2, T], F32)
         gam32 = hold("gam32", [P, 2, T], F32)
         ident_f = hold("ident_f", [P, P], F32)
         ident_b = hold("ident_b", [P, P], BF16)
@@ -63,9 +64,9 @@ def tile_metasgdinnerstepqueryforward_kernel(tc, xs_bytes, xs_scale, zs, delta, 
         xq_s = [hold("xq_s%d" % q, [P, 4, 2, P], U8) for q in range(2)]
         wg_c = [[hold("wg_c%d%d" % (g, h), [P, FH], U32) for h in range(2)] for g in range(2)]
         wg_s = [[hold("wg_s%d%d" % (g, h), [P, FH], U8) for h in range(2)] for g in range(2)]
-        CHUNK = [(0, 0, 512), (1, 0, 512)]
+        CHUNK = [(0, 0, 512), (1, 0, 256), (1, 256, 256)]
 
-        xs_bf, xs_int, hh, r_int, xq_int, tmp, wg_int, g_ps, wp_ps, o_sb = {}, {}, {}, {}, {}, {}, {}, {}, {}, {}
+        xs_bf, xs_int, hh, r_int, xq_int, tmp, wg_int, g_ps, wp_ps, ws = {}, {}, {}, {}, {}, {}, {}, {}, {}, {}
 
         def cols(h):
             return slice(h * FH, (h + 1) * FH)
@@ -84,11 +85,13 @@ def tile_metasgdinnerstepqueryforward_kernel(tc, xs_bytes, xs_scale, zs, delta, 
             load_half(de_t, delta_rows, n, 0)
         load_half(al_t, alpha_rows, 0, 0)
         load_half(w_t, w_rows, 0, 0)
-        for n in range(2):
-            load_half(zs_t, zs_rows, n, 1)
+        load_half(zs_t, zs_rows, 0, 1)
         load_half(al_t, alpha_rows, 1, 0)
+        for q in range(2):
+            nc.sync.dma_start(out=xq_t[q][:], in_=xq_rows[q])
         load_half(w_t, w_rows, 1, 0)
-        for q in range(4):
+        load_half(zs_t, zs_rows, 1, 1)
+        for q in range(2, 4):
             nc.sync.dma_start(out=xq_t[q][:], in_=xq_rows[q])
         for n in range(2):
             load_half(de_t, delta_rows, n, 1)
@@ -103,6 +106,7 @@ def tile_metasgdinnerstepqueryforward_kernel(tc, xs_bytes, xs_scale, zs, delta, 
             nc.scalar.activation(out=warm[:], in_=warm[:], func=ACT.Tanh)
 
         def gamma_columns():
+            nc.vector.tensor_copy(out=gam1[:], in_=gam[:, :, 0:T])
             nc.vector.tensor_scalar(out=gam32[:], in0=gam[:, :, 0:T], scalar1=1.0 / 32.0, scalar2=None, op0=ALU.mult)
 
         def gamma_diagonals():
@@ -145,7 +149,7 @@ def tile_metasgdinnerstepqueryforward_kernel(tc, xs_bytes, xs_scale, zs, delta, 
             nc.vector.quantize_mx(out=xs_c[n][:, c].bitcast(FP8X4), scales=xs_s[n][:, c], in_=src)
 
         def tanh_z(n, h, parts=1):
-            hh[n, h] = ring.tile([P, T, FH], F32, name="hh", bufs=3, align_bytes=64)
+            hh[n, h] = ring.tile([P, T, FH], F32, name="hh", bufs=2, align_bytes=64)
             k = T // parts
             for a in range(parts):
                 t = slice(a * k, (a + 1) * k)
@@ -166,11 +170,12 @@ def tile_metasgdinnerstepqueryforward_kernel(tc, xs_bytes, xs_scale, zs, delta, 
                 out=r_c[n][h][:].bitcast(FP8X4), scales=r_s[n][h][:], in_=r_int[n, h][:].rearrange("p f t -> p (f t)")
             )
 
-        def g_matmul(g, c, t):
+        def g_matmul(g, c, t, ns=(0, 1)):
             h, f0, width = CHUNK[c]
             f = slice(f0, f0 + width)
-            g_ps[g, c, t] = psum.tile([P, width], F32, name="g_ps", bufs=3)
-            for n in range(2):
+            if 0 in ns:
+                g_ps[g, c, t] = psum.tile([P, width], F32, name="g_ps", bufs=3)
+            for n in ns:
                 d0 = (2 * t + g) * P if n == 0 else (4 * g + t) * P
                 d = slice(d0, d0 + P)
                 nc.tensor.matmul_mx(
@@ -178,9 +183,9 @@ def tile_metasgdinnerstepqueryforward_kernel(tc, xs_bytes, xs_scale, zs, delta, 
                     rhs=r_c[n][h][:, f].bitcast(FP8X4), rhs_scale=r_s[n][h][:, f], start=(n == 0), stop=(n == 1),
                 )
 
-        def w_scaled(g, c, j, full=False):
+        def w_scaled(g, c, j, full=False, bank="wp_ps"):
             h, f0, width = CHUNK[c]
-            wp_ps[g, c, j] = psum.tile([P, T, P], F32, name="wp_ps", bufs=2)
+            wp_ps[g, c, j] = psum.tile([P, T, P], F32, name="wp", tag=bank, bufs=3 if bank == "g_ps" else 2)
             for t in range(T):
                 nc.tensor.matmul(
                     wp_ps[g, c, j][:, t, :], lhsT=diag[:, g * T + t, :], rhs=w_t[g][h][:, t, f0 + j * P : f0 + (j + 1) * P],
@@ -211,6 +216,18 @@ def tile_metasgdinnerstepqueryforward_kernel(tc, xs_bytes, xs_scale, zs, delta, 
             nc.vector.tensor_tensor(
                 out=wg_piece(g, c, j).rearrange("p (c i) t -> p c t i", i=RUN),
                 in0=runs(wp_ps[g, c, j][:]), in1=runs(tmp[g, c][:, :, j * P : (j + 1) * P]), op=ALU.add,
+            )
+
+        def w_side(g, c, j):
+            h, f0, width = CHUNK[c]
+            ws[g, c, j] = ring.tile([P, T, P], F32, name="ws", bufs=2, align_bytes=64)
+            for t in range(T):
+                nc.scalar.activation(out=ws[g, c, j][:, t, :], in_=w_t[g][h][:, t, f0 + j * P : f0 + (j + 1) * P], func=ACT.Copy, scale=gam1[:, g, t : t + 1])
+
+        def upd_side(g, c, j):
+            nc.gpsimd.tensor_tensor(
+                out=wg_piece(g, c, j), in0=tmp[g, c][:, :, j * P : (j + 1) * P].rearrange("p t f -> p f t"),
+                in1=ws[g, c, j][:].rearrange("p t f -> p f t"), op=ALU.add,
             )
 
         def upd_out(g, c, j):
@@ -277,93 +294,116 @@ def tile_metasgdinnerstepqueryforward_kernel(tc, xs_bytes, xs_scale, zs, delta, 
         for g in range(2):
             for t in range(2, 4):
                 dequant(1, t, "s", slice(512 * g, 512 * (g + 1)))
+            xs_interleave(1, g, "s")
         r_mul(1, 0)
         r_quant(0, 0)
-        xs_interleave(1, 0)
+        for t in range(3):
+            g_matmul(0, 0, t, (0,))
         r_quant(1, 0)
         xs_quant(1, 0)
         gamma_diagonals()
-        xs_interleave(1, 1, "s")
         tanh_z(0, 1)
         square_z(0, 1)
         for t in range(3):
-            g_matmul(0, 0, t)
+            g_matmul(0, 0, t, (1,))
         w_scaled(0, 0, 0)
         w_scaled(0, 0, 1)
-        upd_mul(0, 0, 0)
-        upd_mul(0, 0, 1)
-        upd_mul(0, 0, 2)
+        for t in range(3):
+            upd_mul(0, 0, t)
         g_matmul(0, 0, 3)
         upd_mul(0, 0, 3)
-        xs_quant(1, 1)
-        for t in range(2):
-            g_matmul(1, 0, t)
-        for t in range(4):
-            upd_add(0, 0, t)
-            if t < 2:
-                w_scaled(0, 0, t + 2)
-                g_matmul(1, 0, t + 2)
-            else:
-                w_scaled(1, 0, t - 2)
-            upd_mul(1, 0, t)
-        for m in range(4):
+        for m in range(3):
             xq_turn(m)
+        xs_quant(1, 1)
+        g_matmul(1, 0, 0)
+        g_matmul(1, 0, 1)
+        upd_add(0, 0, 0)
+        w_scaled(0, 0, 2)
+        upd_add(0, 0, 1)
+        w_scaled(0, 0, 3)
+        upd_mul(1, 0, 0)
+        g_matmul(1, 0, 2)
+        upd_add(0, 0, 2)
+        w_scaled(1, 0, 0)
+        upd_mul(1, 0, 1)
+        g_matmul(1, 0, 3)
+        upd_add(0, 0, 3)
+        w_scaled(1, 0, 1)
+        upd_mul(1, 0, 2)
+        upd_mul(1, 0, 3)
         wg_quant(0, 0, 0, 4)
+        for m in range(3, 6):
+            xq_turn(m)
         for j in range(4):
             upd_add(1, 0, j)
             if j < 2:
                 w_scaled(1, 0, j + 2)
         tanh_z(1, 1)
-        for m in range(4, 8):
+        for m in range(6, 8):
             xq_turn(m)
         square_z(1, 1)
         xq_quant(0)
         wg_quant(1, 0, 0, 4)
         r_mul(0, 1)
+        for m in range(4):
+            out_block(m, 0, 0, 512)
         xq_quant(1)
+        for m in range(4, 6):
+            out_block(m, 0, 0, 512)
         r_quant(0, 1)
+        for t in range(3):
+            g_matmul(0, 1, t, (0,))
         r_mul(1, 1)
-        for m in range(2):
+        for m in range(6, 8):
             out_block(m, 0, 0, 512)
         r_quant(1, 1)
-        for m in range(2, 6):
-            out_block(m, 0, 0, 512)
+        for c in (1, 2):
+            for j in range(2):
+                w_side(0, c, j)
+        w_scaled(1, 1, 0)
+        w_scaled(1, 1, 1)
         for t in range(3):
-            g_matmul(0, 1, t)
-        w_scaled(0, 1, 0)
-        w_scaled(0, 1, 1)
+            g_matmul(0, 1, t, (1,))
         for t in range(4):
             upd_mul(0, 1, t)
             if t == 0:
                 g_matmul(0, 1, 3)
             elif t < 3:
                 g_matmul(1, 1, t - 1)
-        for m in range(6, 8):
-            out_block(m, 0, 0, 512)
+        for j in range(2):
+            upd_side(0, 1, j)
         for t in range(4):
-            if t < 2:
-                upd_add(0, 1, t)
-                w_scaled(1, 1, t)
-                g_matmul(1, 1, t + 2)
             upd_mul(1, 1, t)
-        wg_quant(0, 1, 0, 2)
+            if t < 2:
+                g_matmul(1, 1, t + 2)
+            else:
+                g_matmul(0, 2, t - 2)
+        g_matmul(0, 2, 2)
+        upd_mul(0, 2, 0)
         upd_add(1, 1, 0)
-        w_scaled(0, 1, 2)
-        w_scaled(0, 1, 3)
+        upd_mul(0, 2, 1)
         upd_add(1, 1, 1)
-        upd_add(0, 1, 2)
-        w_scaled(1, 1, 2)
+        g_matmul(0, 2, 3)
+        w_scaled(1, 2, 0)
+        w_scaled(1, 2, 1)
+        upd_mul(0, 2, 2)
+        wg_quant(0, 1, 0, 2)
         wg_quant(1, 1, 0, 2)
-        upd_add(0, 1, 3)
-        w_scaled(1, 1, 3)
-        for m in range(0, 8, 2):
+        upd_mul(0, 2, 3)
+        for j in range(2):
+            upd_side(0, 2, j)
+        for t in range(3):
+            g_matmul(1, 2, t)
+        out_block(0, 1, 0, 256)
+        upd_mul(1, 2, 0)
+        g_matmul(1, 2, 3)
+        for t in range(1, 4):
+            upd_mul(1, 2, t)
+        for m in range(2, 8, 2):
             out_block(m, 1, 0, 256)
-        wg_quant(0, 1, 2, 4)
-        upd_add(1, 1, 2)
-        wg_quant(1, 1, 2, 3)
-        upd_add(1, 1, 3)
-        for m in range(0, 8, 4):
-            out_block(m, 1, 256, 128)
-        wg_quant(1, 1, 3, 4)
-        for m in range(0, 8, 4):
-            out_block(m, 1, 384, 128)
+        upd_add(1, 2, 0)
+        upd_add(1, 2, 1)
+        wg_quant(0, 2, 0, 2)
+        wg_quant(1, 2, 0, 2)
+        for m in range(0, 8, 2):
+            out_block(m, 1, 256, 256)

@@ -131,13 +131,13 @@ def tile_metasgdinnerstepqueryforward_kernel(tc, xs_bytes, xs_scale, zs, delta, 
         def xs_interleave(n, g, engine="v"):
             if n == 0:
                 xs_int[n] = ring.tile([P, D * T], BF16, name="xs_int0", tag="big", bufs=6, align_bytes=64)
-                o = xs_int[n][:].rearrange("p (t m j) -> p m j t", t=T, j=T)
-                i = xs_bf[n][:].rearrange("p j (m t) -> p m j t", t=T)
+                o = xs_int[n][:].rearrange("p (t c b j) -> p c t b j", t=T, b=2, j=T)
+                i = xs_bf[n][:].rearrange("p j (c b t) -> p c t b j", b=2, t=T)
             else:
                 if n not in xs_int:
                     xs_int[n] = ring.tile([P, 2, 512 * T], BF16, name="xs_int1", tag="big", bufs=6, align_bytes=64)
-                o = xs_int[n][:, g, :].rearrange("p (t m j) -> p m j t", t=T, j=T)
-                i = xs_bf[n][:, :, g * 512 : (g + 1) * 512].rearrange("p j (m t) -> p m j t", t=T)
+                o = xs_int[n][:, g, :].rearrange("p (t c b j) -> p c t b j", t=T, b=2, j=T)
+                i = xs_bf[n][:, :, g * 512 : (g + 1) * 512].rearrange("p j (c b t) -> p c t b j", b=2, t=T)
             if engine == "v":
                 nc.vector.tensor_copy(out=o, in_=i)
             else:
@@ -148,7 +148,7 @@ def tile_metasgdinnerstepqueryforward_kernel(tc, xs_bytes, xs_scale, zs, delta, 
             src = xs_int[n][:] if n == 0 else xs_int[n][:, g, :]
             nc.vector.quantize_mx(out=xs_c[n][:, c].bitcast(FP8X4), scales=xs_s[n][:, c], in_=src)
 
-        def tanh_z(n, h, parts=1):
+        def tanh_z(n, h, parts=2):
             hh[n, h] = ring.tile([P, T, FH], F32, name="hh", bufs=2, align_bytes=64)
             k = T // parts
             for a in range(parts):
@@ -156,7 +156,9 @@ def tile_metasgdinnerstepqueryforward_kernel(tc, xs_bytes, xs_scale, zs, delta, 
                 nc.scalar.activation(out=hh[n, h][:, t, :], in_=zs_t[n][h][:, t, :], func=ACT.Tanh)
 
         def square_z(n, h):
-            nc.scalar.activation(out=hh[n, h][:], in_=hh[n, h][:], func=ACT.Square)
+            for a in range(2):
+                x = hh[n, h][:, 2 * a : 2 * a + 2, :]
+                nc.scalar.activation(out=x, in_=x, func=ACT.Square)
 
         def r_mul(n, h):
             r_int[n, h] = ring.tile([P, FH, T], BF16, name="r_int", bufs=2, align_bytes=64)
@@ -357,9 +359,8 @@ def tile_metasgdinnerstepqueryforward_kernel(tc, xs_bytes, xs_scale, zs, delta, 
         for m in range(6, 8):
             out_block(m, 0, 0, 512)
         r_quant(1, 1)
-        for c in (1, 2):
-            for j in range(2):
-                w_side(0, c, j)
+        for c, j in ((1, 0), (1, 1), (2, 0)):
+            w_side(0, c, j)
         w_scaled(1, 1, 0)
         w_scaled(1, 1, 1)
         for t in range(3):
@@ -385,13 +386,12 @@ def tile_metasgdinnerstepqueryforward_kernel(tc, xs_bytes, xs_scale, zs, delta, 
         upd_add(1, 1, 1)
         g_matmul(0, 2, 3)
         w_scaled(1, 2, 0)
-        w_scaled(1, 2, 1)
+        w_scaled(0, 2, 1)
         upd_mul(0, 2, 2)
         wg_quant(0, 1, 0, 2)
         wg_quant(1, 1, 0, 2)
         upd_mul(0, 2, 3)
-        for j in range(2):
-            upd_side(0, 2, j)
+        upd_side(0, 2, 0)
         for t in range(3):
             g_matmul(1, 2, t)
         out_block(0, 1, 0, 256)
@@ -399,7 +399,10 @@ def tile_metasgdinnerstepqueryforward_kernel(tc, xs_bytes, xs_scale, zs, delta, 
         g_matmul(1, 2, 3)
         for t in range(1, 4):
             upd_mul(1, 2, t)
-        for m in range(2, 8, 2):
+        upd_add(0, 2, 1)
+        out_block(2, 1, 0, 256)
+        w_scaled(1, 2, 1)
+        for m in range(4, 8, 2):
             out_block(m, 1, 0, 256)
         upd_add(1, 2, 0)
         upd_add(1, 2, 1)

from contextlib import ExitStack

import concourse.mybir as mybir
from concourse.masks import make_identity

F32 = mybir.dt.float32
BF16 = mybir.dt.bfloat16
U32 = mybir.dt.uint32
U8 = mybir.dt.uint8
FP8 = mybir.dt.float8_e4m3fn
FP8X4 = mybir.dt.float8_e4m3fn_x4
ACT = mybir.ActivationFunctionType
ALU = mybir.AluOpType

N, M, D, F = 1024, 1024, 1024, 1024
P = 128
T = 4
FH = 512
RUN = 4
FLOPS = 2 * N * D * F + 2 * M * D * F


def runs(ap):
    return ap.rearrange("p t (c i) -> p c t i", i=RUN)


def tile_metasgdinnerstepqueryforward_kernel(tc, xs_bytes, xs_scale, zs, delta, xq, w, alpha, gamma, out):
    nc = tc.nc
    xs_rows = xs_bytes.rearrange("(n p t) d -> n p t d", p=P, t=T)
    zs_rows = zs.rearrange("(n p t) f -> n p t f", p=P, t=T)
    delta_rows = delta.rearrange("(n p t) f -> n p t f", p=P, t=T)
    w_rows = w.rearrange("(g p t) f -> g p t f", p=P, t=T)
    alpha_rows = alpha.rearrange("(g p t) f -> g p t f", p=P, t=T)
    xq_rows = xq.rearrange("(q a p) d -> q p a d", a=2, p=P)

    with ExitStack() as ctx:
        keep = ctx.enter_context(tc.tile_pool(name="keep", bufs=1))
        ring = ctx.enter_context(tc.tile_pool(name="ring", bufs=2))
        psum = ctx.enter_context(tc.psum_pool(name="psum", bufs=2))
        ctx.enter_context(tc.manual_schedule())

        def hold(name, shape, dtype):
            return keep.tile(shape, dtype, name=name, align_bytes=64)

        scale = hold("scale", [P, 2, 8], F32)
        gam = hold("gam", [P, 2, 16], BF16)
        gam1 = hold("gam1", [P, 2, T], F32)
        gam32 = hold("gam32", [P, 2, T], F32)
        ident_f = hold("ident_f", [P, P], F32)
        ident_b = hold("ident_b", [P, P], BF16)
        diag = hold("diag", [P, 2 * T, P], BF16)
        warm = hold("warm", [P, 1], F32)
        xs_b = [hold("xs_b%d" % n, [P, T, D], U8) for n in range(2)]
        zs_t = [[hold("zs%d%d" % (n, h), [P, T, FH], BF16) for h in range(2)] for n in range(2)]
        de_t = [[hold("de%d%d" % (n, h), [P, T, FH], BF16) for h in range(2)] for n in range(2)]
        al_t = [[hold("al%d%d" % (g, h), [P, T, FH], BF16) for h in range(2)] for g in range(2)]
        w_t = [[hold("w%d%d" % (g, h), [P, T, FH], BF16) for h in range(2)] for g in range(2)]
        xq_t = [hold("xq%d" % q, [P, 2, D], BF16) for q in range(4)]
        xs_c = [hold("xs_c%d" % n, [P, D], U32) for n in range(2)]
        xs_s = [hold("xs_s%d" % n, [P, D], U8) for n in range(2)]
        r_c = [[hold("r_c%d%d" % (n, h), [P, FH], U32) for h in range(2)] for n in range(2)]
        r_s = [[hold("r_s%d%d" % (n, h), [P, FH], U8) for h in range(2)] for n in range(2)]
        xq_c = [hold("xq_c%d" % q, [P, 4, 2, P], U32) for q in range(2)]
        xq_s = [hold("xq_s%d" % q, [P, 4, 2, P], U8) for q in range(2)]
        wg_c = [[hold("wg_c%d%d" % (g, h), [P, FH], U32) for h in range(2)] for g in range(2)]
        wg_s = [[hold("wg_s%d%d" % (g, h), [P, FH], U8) for h in range(2)] for g in range(2)]
        CHUNK = [(0, 0, 512), (1, 0, 256), (1, 256, 256)]

        xs_bf, xs_int, hh, r_int, xq_int, tmp, wg_int, g_ps, wp_ps, ws = {}, {}, {}, {}, {}, {}, {}, {}, {}, {}

        def cols(h):
            return slice(h * FH, (h + 1) * FH)

        def load_half(tiles, rows, n, h):
            nc.sync.dma_start(out=tiles[n][h][:], in_=rows[n][:, :, cols(h)])

        nc.scalar.dma_start(out=scale[:, :, 0:T], in_=xs_scale.rearrange("(n p t) o -> p n (t o)", p=P, t=T))
        nc.scalar.dma_start(out=gam[:, :, 0:T], in_=gamma.rearrange("(g p t) -> p g t", p=P, t=T))
        for t in (slice(0, 2), slice(2, 4)):
            nc.sync.dma_start(out=xs_b[0][:, t, :], in_=xs_rows[0][:, t, :])
            nc.sync.dma_start(out=zs_t[0][0][:, t, :], in_=zs_rows[0][:, t, cols(0)])
        nc.sync.dma_start(out=xs_b[1][:], in_=xs_rows[1])
        load_half(zs_t, zs_rows, 1, 0)
        for n in range(2):
            load_half(de_t, delta_rows, n, 0)
        load_half(al_t, alpha_rows, 0, 0)
        load_half(w_t, w_rows, 0, 0)
        load_half(zs_t, zs_rows, 0, 1)
        load_half(al_t, alpha_rows, 1, 0)
        for q in range(2):
            nc.sync.dma_start(out=xq_t[q][:], in_=xq_rows[q])
        load_half(w_t, w_rows, 1, 0)
        load_half(zs_t, zs_rows, 1, 1)
        for q in range(2, 4):
            nc.sync.dma_start(out=xq_t[q][:], in_=xq_rows[q])
        for n in range(2):
            load_half(de_t, delta_rows, n, 1)
        for g in range(2):
            load_half(al_t, alpha_rows, g, 1)
            load_half(w_t, w_rows, g, 1)

        def setup():
            nc.gpsimd.memset(warm[:], 0.0)
            make_identity(nc, ident_f[:])
            make_identity(nc, ident_b[:])
            nc.scalar.activation(out=warm[:], in_=warm[:], func=ACT.Tanh)

        def gamma_columns():
            nc.vector.tensor_copy(out=gam1[:], in_=gam[:, :, 0:T])
            nc.vector.tensor_scalar(out=gam32[:], in0=gam[:, :, 0:T], scalar1=1.0 / 32.0, scalar2=None, op0=ALU.mult)

        def gamma_diagonals():
            nc.vector.tensor_tensor(
                out=diag[:].rearrange("p (g t) c -> p g t c", g=2),
                in0=ident_b[:].unsqueeze(1).unsqueeze(1).to_broadcast([P, 2, T, P]),
                in1=gam[:, :, 0:T].unsqueeze(3).to_broadcast([P, 2, T, P]),
                op=ALU.mult,
            )

        def dequant(n, t, engine, d=slice(0, D)):
            if n not in xs_bf:
                xs_bf[n] = ring.tile([P, T, D], BF16, name="xs_bf", tag="big", bufs=6, align_bytes=64)
            src = xs_b[n][:, t, d].bitcast(FP8)
            dst = xs_bf[n][:, t, d]
            col = scale[:, n, t : t + 1]
            if engine == "v":
                nc.vector.tensor_scalar(out=dst, in0=src, scalar1=col, scalar2=None, op0=ALU.mult)
            else:
                nc.scalar.activation(out=dst, in_=src, func=ACT.Copy, scale=col)

        def xs_interleave(n, g, engine="v"):
            if n == 0:
                xs_int[n] = ring.tile([P, D * T], BF16, name="xs_int0", tag="big", bufs=6, align_bytes=64)
                o = xs_int[n][:].rearrange("p (t c b j) -> p c t b j", t=T, b=2, j=T)
                i = xs_bf[n][:].rearrange("p j (c b t) -> p c t b j", b=2, t=T)
            else:
                if n not in xs_int:
                    xs_int[n] = ring.tile([P, 2, 512 * T], BF16, name="xs_int1", tag="big", bufs=6, align_bytes=64)
                o = xs_int[n][:, g, :].rearrange("p (t c b j) -> p c t b j", t=T, b=2, j=T)
                i = xs_bf[n][:, :, g * 512 : (g + 1) * 512].rearrange("p j (c b t) -> p c t b j", b=2, t=T)
            if engine == "v":
                nc.vector.tensor_copy(out=o, in_=i)
            else:
                nc.scalar.copy(out=o, in_=i)

        def xs_quant(n, g):
            c = slice(0, D) if n == 0 else slice(g * 512, (g + 1) * 512)
            src = xs_int[n][:] if n == 0 else xs_int[n][:, g, :]
            nc.vector.quantize_mx(out=xs_c[n][:, c].bitcast(FP8X4), scales=xs_s[n][:, c], in_=src)

        def tanh_z(n, h, parts=2):
            hh[n, h] = ring.tile([P, T, FH], F32, name="hh", bufs=2, align_bytes=64)
            k = T // parts
            for a in range(parts):
                t = slice(a * k, (a + 1) * k)
                nc.scalar.activation(out=hh[n, h][:, t, :], in_=zs_t[n][h][:, t, :], func=ACT.Tanh)

        def square_z(n, h):
            for a in range(2):
                x = hh[n, h][:, 2 * a : 2 * a + 2, :]
                nc.scalar.activation(out=x, in_=x, func=ACT.Square)

        def r_mul(n, h):
            r_int[n, h] = ring.tile([P, FH, T], BF16, name="r_int", bufs=2, align_bytes=64)
            nc.vector.scalar_tensor_tensor(
                out=r_int[n, h][:], in0=hh[n, h][:].rearrange("p t f -> p f t"), scalar=1.0,
                in1=de_t[n][h][:].rearrange("p t f -> p f t"), op0=ALU.subtract, op1=ALU.mult,
            )

        def r_quant(n, h):
            nc.vector.quantize_mx(
                out=r_c[n][h][:].bitcast(FP8X4), scales=r_s[n][h][:], in_=r_int[n, h][:].rearrange("p f t -> p (f t)")
            )

        def g_matmul(g, c, t, ns=(0, 1)):
            h, f0, width = CHUNK[c]
            f = slice(f0, f0 + width)
            if 0 in ns:
                g_ps[g, c, t] = psum.tile([P, width], F32, name="g_ps", bufs=3)
            for n in ns:
                d0 = (2 * t + g) * P if n == 0 else (4 * g + t) * P
                d = slice(d0, d0 + P)
                nc.tensor.matmul_mx(
                    out=g_ps[g, c, t][:], lhsT=xs_c[n][:, d].bitcast(FP8X4), lhsT_scale=xs_s[n][:, d],
                    rhs=r_c[n][h][:, f].bitcast(FP8X4), rhs_scale=r_s[n][h][:, f], start=(n == 0), stop=(n == 1),
                )

        def w_scaled(g, c, j, full=False, bank="wp_ps"):
            h, f0, width = CHUNK[c]
            wp_ps[g, c, j] = psum.tile([P, T, P], F32, name="wp", tag=bank, bufs=3 if bank == "g_ps" else 2)
            for t in range(T):
                nc.tensor.matmul(
                    wp_ps[g, c, j][:, t, :], lhsT=diag[:, g * T + t, :], rhs=w_t[g][h][:, t, f0 + j * P : f0 + (j + 1) * P],
                    start=True, stop=not full,
                )
                if full:
                    nc.tensor.matmul(
                        wp_ps[g, c, j][:, t, :], lhsT=ident_f[:], rhs=tmp[g, c][:, t, j * P : (j + 1) * P],
                        start=False, stop=True,
                    )

        def upd_mul(g, c, t):
            h, f0, width = CHUNK[c]
            if t == 0:
                tmp[g, c] = ring.tile([P, T, width], F32, name="tmp", tag="big", bufs=6, align_bytes=64)
            nc.vector.scalar_tensor_tensor(
                out=tmp[g, c][:, t, :], in0=g_ps[g, c, t][:], scalar=gam32[:, g, t : t + 1],
                in1=al_t[g][h][:, t, f0 : f0 + width], op0=ALU.mult, op1=ALU.mult,
            )

        def wg_piece(g, c, j):
            h, f0, width = CHUNK[c]
            if (g, c) not in wg_int:
                wg_int[g, c] = ring.tile([P, width, T], BF16, name="wg_int", bufs=2, align_bytes=64)
            return wg_int[g, c][:, j * P : (j + 1) * P, :]

        def upd_add(g, c, j):
            nc.vector.tensor_tensor(
                out=wg_piece(g, c, j).rearrange("p (c i) t -> p c t i", i=RUN),
                in0=runs(wp_ps[g, c, j][:]), in1=runs(tmp[g, c][:, :, j * P : (j + 1) * P]), op=ALU.add,
            )

        def w_side(g, c, j):
            h, f0, width = CHUNK[c]
            ws[g, c, j] = ring.tile([P, T, P], F32, name="ws", bufs=2, align_bytes=64)
            for t in range(T):
                nc.scalar.activation(out=ws[g, c, j][:, t, :], in_=w_t[g][h][:, t, f0 + j * P : f0 + (j + 1) * P], func=ACT.Copy, scale=gam1[:, g, t : t + 1])

        def upd_side(g, c, j):
            nc.gpsimd.tensor_tensor(
                out=wg_piece(g, c, j), in0=tmp[g, c][:, :, j * P : (j + 1) * P].rearrange("p t f -> p f t"),
                in1=ws[g, c, j][:].rearrange("p t f -> p f t"), op=ALU.add,
            )

        def upd_out(g, c, j):
            nc.scalar.copy(out=wg_piece(g, c, j), in_=wp_ps[g, c, j][:].rearrange("p t f -> p f t"))

        def wg_quant(g, c, j0, j1):
            h, f0, width = CHUNK[c]
            f = slice(f0 + j0 * P, f0 + j1 * P)
            nc.vector.quantize_mx(
                out=wg_c[g][h][:, f].bitcast(FP8X4), scales=wg_s[g][h][:, f],
                in_=wg_int[g, c][:, j0 * P : j1 * P, :].rearrange("p f t -> p (f t)"),
            )

        def xq_turn(m):
            q, a = divmod(m, 4)
            bank = psum.tile([P, 2, 2, P], F32, name="o_ps", bufs=3)
            words = xq_t[m // 2][:, m % 2, :].bitcast(F32)
            for g in range(2):
                for u in range(2):
                    nc.tensor.transpose(bank[:, g, u, :], words[:, 256 * g + u : 256 * (g + 1) : 2], ident_f[:])
            if a == 0:
                xq_int[q] = ring.tile([P, 4, 2, P, T], BF16, name="xq_int", tag="big", bufs=6, align_bytes=64)
            nc.scalar.copy(
                out=xq_int[q][:, a].rearrange("p g r t -> p (g r t)").bitcast(F32).rearrange("p (g r u) -> p g r u", g=2, u=2),
                in_=bank[:].rearrange("p g u r -> p g r u"),
            )

        def xq_quant(q):
            nc.vector.quantize_mx(
                out=xq_c[q][:].rearrange("p a g r -> p (a g r)").bitcast(FP8X4),
                scales=xq_s[q][:].rearrange("p a g r -> p (a g r)"),
                in_=xq_int[q][:].rearrange("p a g r t -> p (a g r t)"),
            )

        def out_block(m0, h, f0, width):
            k = 512 // width
            bank = psum.tile([P, k, width], F32, name="o_ps", bufs=3)
            f = slice(f0, f0 + width)
            for b in range(k):
                q, a = divmod(m0 + b, 4)
                for g in range(2):
                    nc.tensor.matmul_mx(
                        out=bank[:, b, :], lhsT=xq_c[q][:, a, g, :].bitcast(FP8X4), lhsT_scale=xq_s[q][:, a, g, :],
                        rhs=wg_c[g][h][:, f].bitcast(FP8X4), rhs_scale=wg_s[g][h][:, f], start=(g == 0), stop=(g == 1),
                    )
            res = ring.tile([P, k, width], F32, name="res", bufs=8, align_bytes=64)
            nc.scalar.activation(out=res[:], in_=bank[:], func=ACT.Tanh)
            rows = out[m0 * P : (m0 + k) * P, h * FH + f0 : h * FH + f0 + width]
            nc.sync.dma_start(out=rows.rearrange("(b p) f -> p b f", p=P), in_=res[:])

        setup()
        tanh_z(0, 0, 2)
        square_z(0, 0)
        for t in range(4):
            dequant(0, t, "v")
        xs_interleave(0, 0)
        dequant(1, 0, "v")
        dequant(1, 1, "v")
        xs_quant(0, 0)
        gamma_columns()
        tanh_z(1, 0)
        square_z(1, 0)
        r_mul(0, 0)
        for g in range(2):
            for t in range(2, 4):
                dequant(1, t, "s", slice(512 * g, 512 * (g + 1)))
            xs_interleave(1, g, "s")
        r_mul(1, 0)
        r_quant(0, 0)
        for t in range(3):
            g_matmul(0, 0, t, (0,))
        r_quant(1, 0)
        xs_quant(1, 0)
        gamma_diagonals()
        tanh_z(0, 1)
        square_z(0, 1)
        for t in range(3):
            g_matmul(0, 0, t, (1,))
        w_scaled(0, 0, 0)
        w_scaled(0, 0, 1)
        for t in range(3):
            upd_mul(0, 0, t)
        g_matmul(0, 0, 3)
        upd_mul(0, 0, 3)
        for m in range(3):
            xq_turn(m)
        xs_quant(1, 1)
        g_matmul(1, 0, 0)
        g_matmul(1, 0, 1)
        upd_add(0, 0, 0)
        w_scaled(0, 0, 2)
        upd_add(0, 0, 1)
        w_scaled(0, 0, 3)
        upd_mul(1, 0, 0)
        g_matmul(1, 0, 2)
        upd_add(0, 0, 2)
        w_scaled(1, 0, 0)
        upd_mul(1, 0, 1)
        g_matmul(1, 0, 3)
        upd_add(0, 0, 3)
        w_scaled(1, 0, 1)
        upd_mul(1, 0, 2)
        upd_mul(1, 0, 3)
        wg_quant(0, 0, 0, 4)
        for m in range(3, 6):
            xq_turn(m)
        for j in range(4):
            upd_add(1, 0, j)
            if j < 2:
                w_scaled(1, 0, j + 2)
        tanh_z(1, 1)
        for m in range(6, 8):
            xq_turn(m)
        square_z(1, 1)
        xq_quant(0)
        wg_quant(1, 0, 0, 4)
        r_mul(0, 1)
        for m in range(4):
            out_block(m, 0, 0, 512)
        xq_quant(1)
        for m in range(4, 6):
            out_block(m, 0, 0, 512)
        r_quant(0, 1)
        for t in range(3):
            g_matmul(0, 1, t, (0,))
        r_mul(1, 1)
        for m in range(6, 8):
            out_block(m, 0, 0, 512)
        r_quant(1, 1)
        for c, j in ((1, 0), (1, 1), (2, 0)):
            w_side(0, c, j)
        w_scaled(1, 1, 0)
        w_scaled(1, 1, 1)
        for t in range(3):
            g_matmul(0, 1, t, (1,))
        for t in range(4):
            upd_mul(0, 1, t)
            if t == 0:
                g_matmul(0, 1, 3)
            elif t < 3:
                g_matmul(1, 1, t - 1)
        for j in range(2):
            upd_side(0, 1, j)
        for t in range(4):
            upd_mul(1, 1, t)
            if t < 2:
                g_matmul(1, 1, t + 2)
            else:
                g_matmul(0, 2, t - 2)
        g_matmul(0, 2, 2)
        upd_mul(0, 2, 0)
        upd_add(1, 1, 0)
        upd_mul(0, 2, 1)
        upd_add(1, 1, 1)
        g_matmul(0, 2, 3)
        w_scaled(1, 2, 0)
        w_scaled(0, 2, 1)
        upd_mul(0, 2, 2)
        wg_quant(0, 1, 0, 2)
        wg_quant(1, 1, 0, 2)
        upd_mul(0, 2, 3)
        upd_side(0, 2, 0)
        for t in range(3):
            g_matmul(1, 2, t)
        out_block(0, 1, 0, 256)
        upd_mul(1, 2, 0)
        g_matmul(1, 2, 3)
        for t in range(1, 4):
            upd_mul(1, 2, t)
        upd_add(0, 2, 1)
        out_block(2, 1, 0, 256)
        w_scaled(1, 2, 1)
        for m in range(4, 8, 2):
            out_block(m, 1, 0, 256)
        upd_add(1, 2, 0)
        upd_add(1, 2, 1)
        wg_quant(0, 2, 0, 2)
        wg_quant(1, 2, 0, 2)
        for m in range(0, 8, 2):
            out_block(m, 1, 256, 256)
